import numpy as np, ml_dtypes
CORES = [24,25,26,27,28,29,30,31]
N = 8
BF = ml_dtypes.bfloat16
def gentries(a):
    return np.ascontiguousarray(a.reshape(8, 16, -1).transpose(0, 2, 1)).reshape(8, -1)
def gtable(e):
    e = np.asarray(e); return np.ascontiguousarray(e.reshape(8, -1, 16).transpose(0, 2, 1)).reshape(128, -1).astype(np.int32)
IT, M, CAP, ST, RO = 4096, 1024, 128, 6, 2
def forest(rng):
    k = np.full((N, 8, 2, M), M, np.int64); par = np.zeros((N, 8, M), np.int64); m = M // 8
    for q in range(N):
        for g in range(8):
            p = rng.permutation(M).reshape(8, m); par[q, g, p[1::2].reshape(-1)] = 1
            for l in range(7):
                u = rng.permutation(2 * m)[:m]; k[q, g, u // m, p[l, u % m]] = p[l + 1]
    return k, par
def labels(rng, e):
    lab = np.full((N, 8, IT), M, np.int64)
    for q in range(N):
        for g in range(8):
            n = int(e[q, g]); live = rng.permutation(M)[:n]; o = rng.permutation(IT)
            w = live[np.minimum((n * rng.random(IT - n) ** 2).astype(np.int64), n - 1)]
            lab[q, g, o[:n]] = live; lab[q, g, o[n:]] = np.where(rng.random(IT - n) < 0.06, M, w)
    return lab
def lot(rng, live):
    o = rng.permutation(IT); n = len(live); lab = np.full(IT, M, np.int64)
    lab[o[:n]] = live; lab[o[n:]] = np.where(rng.random(IT - n) < 0.06, M, live[rng.integers(0, n, IT - n)])
    return lab
def count(rng):
    return rng.integers(M * 5 // 8, M * 7 // 8, (N, 8))
def parts(rng, lab=None):
    if lab is None: lab = labels(rng, count(rng))
    k, par = forest(rng); n = np.zeros((N, 8, IT), np.int64); cur = np.zeros((N, 8, M), np.int64); siz = np.zeros((N, 8, M), np.int64)
    for q in range(N):
        for g in range(8):
            o = rng.permutation(IT); o = o[np.argsort(lab[q, g, o], kind="stable")]; s = lab[q, g, o]
            last = np.append(s[1:] != s[:-1], True)
            n[q, g, o] = np.where(last, o[np.searchsorted(s, s)], np.roll(o, -1))
            z = np.bincount(s, minlength=M + 1)[:M]; a = np.minimum(np.searchsorted(s, np.arange(M)), IT - 1)
            siz[q, g] = z; cur[q, g] = np.where(z > 0, o[a], rng.integers(0, IT, M))
    tgt = np.minimum(np.maximum(siz + rng.integers(-2, 4, siz.shape), 0), IT)
    return {"k": k, "par": par, "n": n, "cur": cur, "siz": siz, "tgt": tgt}
def values(rng):
    h = rng.choice(np.array([60, 90, 140, 230]), (N, 8, 1, 1))
    x = np.clip(rng.integers(40, 215, (N, 8, 1, IT)) + rng.integers(-40, 41, (N, 8, 16, IT)), 0, 254)
    key = np.clip((h * rng.random((N, 8, 1, M))).astype(np.int64) + rng.integers(-40, 41, (N, 8, 16, M)), 0, 254)
    return x, key
def pack(d, x, key):
    tab = lambda a: np.stack([gtable(b) for b in a])
    key = np.where(d["siz"][:, :, None, :] > 0, key, 255)
    return {"x": np.ascontiguousarray(x.reshape(N, 128, IT)).astype(np.float32).astype(BF), "ky": np.ascontiguousarray(key.reshape(N, 128, M)).astype(np.float32).astype(BF),
            "nxt": d["n"].astype(np.int32), "cur": tab(d["cur"]), "siz": tab(d["siz"]), "tgt": tab(d["tgt"]), "par": tab(d["par"]), "kl": tab(d["k"][:, :, 0]), "kr": tab(d["k"][:, :, 1])}
def setup_inputs(rng):
    d = parts(rng); x, key = values(rng)
    return pack(d, x, key)
def setup_inputs_room(rng):
    d = parts(rng); d["tgt"] = np.where(d["par"] == 0, 0, d["tgt"])
    x = rng.integers(40, 201, (N, 8, 16, IT)); key = rng.integers(0, 40, (N, 8, 16, M))
    for q in range(N):
        for g in range(8):
            live = rng.permutation(np.nonzero(d["siz"][q, g])[0]); e = len(live)
            n = int(rng.choice(np.array([0, 1, CAP - 1, CAP, CAP + 1, e])))
            if q == 0: n = (CAP, CAP + 1, e, CAP - 1, 1, 0, CAP, CAP + 1)[g]
            if q == 1: n = (CAP + 1, CAP, CAP, e, CAP, CAP, 0, 1)[g]
            key[q, g][:, live[:n]] = rng.integers(201, 255, (16, n))
    return pack(d, x, key)
def setup_inputs_ties(rng):
    d = parts(rng); c = np.array([0, 7, 8, 9, 16])
    place = np.argsort(rng.random((N, 8, 16, 1)), axis=2)
    a = rng.choice(c, (N, 8, 1, IT)); w = rng.integers(1, 100, (N, 8, 16, IT)) * (rng.random((N, 8, 1, IT)) < 0.8)
    x = np.where(place < a, 100 - w, 100 + w)
    key = 100 + (place < rng.choice(c, (N, 8, 1, M))).astype(np.int64); key[:, ::2] = 100
    return pack(d, x, key)
def setup_inputs_ends(rng):
    e = count(rng); e[:, 2] = M; e[:, 3] = M // 16; lab = labels(rng, e)
    for q in range(N):
        n = int(e[q, 0]); lab[q, 0] = M; lab[q, 0, rng.permutation(IT)[:n]] = rng.permutation(M)[:n]
        live = rng.permutation(M)[:M // 4]; lab[q, 1] = live[0]; lab[q, 1, rng.permutation(IT)[:M // 4]] = live
    d = parts(rng, lab); d["k"][:, 4, 0] = M; d["k"][:, 5, 1] = M; h = M // 2
    for q in range(N):
        a = rng.permutation(M); d["k"][q, 7] = M; d["k"][q, 7, 0, a[:h]] = a[h:]; d["k"][q, 7, 1, a[h:]] = a[:h]
        d["par"][q, 7, a[:h]] = 0; d["par"][q, 7, a[h:]] = 1
        for g, b in ((4, 0), (5, 1)):
            k = d["k"][q, g]; lone = np.all(k == M, axis=0); lone[k[k < M]] = False; d["par"][q, g, lone] = b
    z = d["siz"]; u = rng.integers(0, 4, z.shape); big = np.argmax(z[:, 1], axis=1); r = np.arange(N)
    for q in range(N):
        w = np.nonzero((z[q, 1] > 0) & (d["par"][q, 1] != d["par"][q, 1, big[q]]))[0]
        if len(w) > 0:
            w = int(rng.choice(w)); k = d["k"][q, 1]; k[(k == big[q]) | (k == w)] = M
            k[0, big[q]] = w; k[1, big[q]] = M
    d["tgt"] = np.where(u == 0, 0, np.where(u == 1, z, np.where(u == 2, np.minimum(z + 1, IT), IT)))
    d["tgt"][r, 1, big] = z[r, 1, big] + 1 - r % 2
    x, key = values(rng)
    return pack(d, x, key)
def setup_inputs_full(rng):
    h = M // 2; m = M // 4; lab = labels(rng, count(rng)); a = np.argsort(rng.random((N, 8, M)), axis=2); top = np.zeros((N, 5), np.int64)
    for q in range(N):
        for g, w in ((0, a[q, 0]), (1, a[q, 1, h:]), (2, a[q, 2]), (3, a[q, 3]), (4, np.concatenate([a[q, 4, :m // 2], a[q, 4, m:2 * m], a[q, 4, 3 * m:]]))):
            lab[q, g] = lot(rng, w)
        lab[q, 5] = a[q, 5, 1]; lab[q, 5, rng.permutation(IT)[:(IT - 1, IT, IT - 1, IT - 2)[q % 4]]] = a[q, 5, 0]
        lab[q, 6] = a[q, 6, 15:][rng.integers(0, M - 15, IT)]; o = rng.permutation(IT); at = 0
        for f in range(5):
            kid = int(rng.integers(1, 41)); s = IT // 8 + 45 + 4 * int(rng.integers(0, 14)) + 2 * (f % 2); top[q, f] = s + f % 2
            for v, n in ((f, s - kid), (5 + f, kid), (10 + f, kid)):
                lab[q, 6, o[at:at + n]] = a[q, 6, v]; at += n
    d = parts(rng, lab); k, par, t, z = d["k"], d["par"], d["tgt"], d["siz"]; k[:, :7] = M
    x, key = values(rng)
    for g in (0, 1, 2, 4): t[:, g] = np.minimum(z[:, g] + rng.integers(1, 50, (N, M)), IT)
    x[:, 3] = rng.integers(40, 201, (N, 16, IT)); key[:, 3] = rng.integers(0, 40, (N, 16, M))
    x[:, 4] = np.where(rng.random((N, 1, IT)) < 0.3, 254, rng.integers(200, 255, (N, 16, IT)))
    for q in range(N):
        for g in (0, 1):
            b = (q + g) % 2; k[q, g, rng.integers(0, 2, h), a[q, g, :h]] = a[q, g, h:]
            par[q, g, a[q, g, :h]] = b; par[q, g, a[q, g, h:]] = 1 - b
        w = rng.permutation(M - 16)[:16]; k[q, 2, rng.integers(0, 2, 16), np.arange(M - 16, M)] = w
        par[q, 2] = q % 2; par[q, 2, w] = 1 - q % 2
        key[q, 3][:, int(rng.integers(0, 16))::16] = rng.integers(201, 255, (16, M // 16))
        p = a[q, 4]; b = (q // 2) % 2; k[q, 4, 1, p[:m]] = p[m:2 * m]; k[q, 4, 0, p[:m:2]] = p[2 * m:3 * m:2]
        par[q, 4, p[:m]] = b; par[q, 4, p[m:3 * m]] = 1 - b
        c = np.where(rng.random(m) < 0.5, 16, rng.integers(9, 17, m)); place = np.argsort(rng.random((16, m)), axis=0)
        key[q, 4][:, p[m:2 * m]] = np.where(place < c, 254, rng.integers(100, 255, (16, m)))
        key[q, 4][:, p[3 * m:3 * m + m // 2]] = 254
        b = int(rng.integers(0, 2)); u, w = int(a[q, 5, 0]), int(a[q, 5, 1]); k[q, 5, int(rng.integers(0, 2)), u] = w
        par[q, 5, u] = b; par[q, 5, w] = 1 - b; t[q, 5, u] = (IT, IT, IT - 1, IT - 1)[q % 4]
        p = a[q, 6]; k[q, 6, 0, p[:5]] = p[5:10]; k[q, 6, 1, p[:5]] = p[10:15]
        par[q, 6, p[:5]] = 0; par[q, 6, p[5:15]] = 1; t[q, 6, p[:5]] = top[q]
    return pack(d, x, key)
def setup_inputs_spread(rng):
    d = parts(rng)
    d["tgt"] = np.minimum(np.exp2(13 * rng.random((N, 8, M))).astype(np.int64) - 1, IT)
    x = np.minimum((np.exp2(8 * rng.random((N, 8, 1, IT))) * rng.random((N, 8, 16, IT))).astype(np.int64), 254)
    key = np.minimum((np.exp2(8 * rng.random((N, 8, 1, M))) * rng.random((N, 8, 16, M))).astype(np.int64), 254)
    return pack(d, x, key)
def check_inputs(d):
    bad = []
    for k, hi in (("x", 254), ("ky", 255)):
        a = np.asarray(d[k]).astype(np.float32)
        if not np.all((a >= 0) & (a <= hi) & (a == np.floor(a))): bad.append("whole numbers and range of " + k)
    for k, hi in (("nxt", IT - 1), ("cur", IT - 1), ("siz", IT), ("tgt", IT), ("par", 1), ("kl", M), ("kr", M)):
        if np.min(d[k]) < 0 or np.max(d[k]) > hi: bad.append("range of " + k)
    if bad: return bad
    n = np.asarray(d["nxt"]).astype(np.int64)
    if np.any(np.sort(n, axis=2) != np.arange(IT)): return ["every item once in a row of nxt"]
    cur, siz, par, kl, kr = [np.stack([gentries(a) for a in d[k]]).astype(np.int64) for k in ("cur", "siz", "par", "kl", "kr")]
    live = siz > 0; key = np.asarray(d["ky"]).astype(np.float32).reshape(N, 8, 16, M)
    if np.any(np.where(live[:, :, None, :], key > 254, key != 255)): bad.append("keys of empty and of other nodes")
    lab = np.tile(np.arange(IT), (N, 8, 1)); j = n
    for i in range((IT - 1).bit_length()):
        lab = np.minimum(lab, np.take_along_axis(lab, j, 2)); j = np.take_along_axis(j, j, 2)
    def tally(a, w, k):
        a = (a + np.arange(N * 8).reshape(N, 8, 1) * k)[w]
        return np.bincount(a, minlength=N * 8 * k).reshape(N, 8, k)
    c = tally(lab, np.ones(lab.shape, bool), IT); own = np.take_along_axis(lab, cur, 2)
    if np.any(live & (np.take_along_axis(c, own, 2) != siz)): bad.append("sizes are the rings' numbers of items")
    if np.max(tally(own, live, IT)) > 1: bad.append("nodes that aren't empty have different rings")
    kids = np.concatenate([kl, kr], axis=2)
    if np.max(tally(kids, kids < M, M)) > 1: bad.append("a node stands at most once in kl and kr")
    px = np.concatenate([par, np.full((N, 8, 1), 2, np.int64)], axis=2)
    if np.any(np.take_along_axis(px, kids, 2) == np.concatenate([par, par], axis=2)): bad.append("parities of kids")
    return bad
def reference(x, ky, nxt, cur, siz, tgt, par, kl, kr):
    X = x.astype(np.float32).reshape(N, 8, 16, IT)
    K = np.concatenate([ky.astype(np.float32).reshape(N, 8, 16, M), np.full((N, 8, 16, 1), 255, np.float32)], axis=3)
    nx = nxt.astype(np.int64)
    C, Z, T, P, A, B = [np.stack([gentries(a) for a in b]).astype(np.int64) for b in (cur, siz, tgt, par, kl, kr)]
    none = np.zeros((N, 8, 1), np.int64); C = np.concatenate([C, none], axis=2); Z = np.concatenate([Z, none], axis=2)
    for t in range(RO):
        le = np.take_along_axis(K, A[:, :, None, :], 3) <= np.take_along_axis(K, B[:, :, None, :], 3)
        ch = np.where(np.add.reduce(le, axis=2, dtype=np.int64) >= 9, A, B)
        go = (P == t % 2) & (Z[..., :M] < T) & (np.take_along_axis(Z, ch, 2) > 0)
        i, j, v = np.nonzero(go & (Z[..., :M] > 0)); c = ch[i, j, v]
        a, b = C[i, j, v], C[i, j, c]; na, nb = nx[i, j, a], nx[i, j, b]
        nx[i, j, a] = nb; nx[i, j, b] = na
        i, j, v = np.nonzero(go); c = ch[i, j, v]
        C[i, j, v] = np.where(Z[i, j, v] > 0, C[i, j, v], C[i, j, c])
        K[i, j, :, v] = K[i, j, :, c]; K[i, j, :, c] = 255
        Z[i, j, v] = Z[i, j, v] + Z[i, j, c]; Z[i, j, c] = 0
        live = Z[..., :M] > 0; s = C[..., :M]; lv = np.full((N, 8, M), -1, np.int64)
        for k in range(ST):
            s = np.take_along_axis(nx, s, 2)
            low = np.take_along_axis(X, s[:, :, None, :], 3) < K[..., :M]
            lv = np.where((lv < 0) & live & (np.add.reduce(low, axis=2, dtype=np.int64) >= 9), s, lv)
        C[..., :M] = np.where(live, s, C[..., :M])
        has = (lv >= 0).astype(np.int64); pl = np.add.accumulate(has, axis=2) - 1
        i, j, v = np.nonzero((has == 1) & (pl < CAP))
        e = np.full((N, 8, CAP), -1, np.int64); e[i, j, pl[i, j, v]] = lv[i, j, v]
        come = np.roll(np.take_along_axis(X, np.maximum(e, 0)[:, :, None, :], 3), 1, axis=0)
        i, j, k = np.nonzero((e >= 0) & (np.roll(e, 1, axis=0) >= 0))
        X[i, j, :, e[i, j, k]] = come[i, j, :, k]
    return {"yx": X.reshape(N, 128, IT).astype(BF), "yk": np.ascontiguousarray(K[..., :M]).reshape(N, 128, M).astype(BF), "yn": nx.astype(np.float32),
            "yc": np.stack([gtable(a) for a in np.ascontiguousarray(C[..., :M])]).astype(np.float32)}

from concourse.mybir import AluOpType as A, ActivationFunctionType as F

BF, F32, I32, U16, F16 = "bfloat16", "float32", "int32", "uint16", "float16"
SCRATCH = {
    "NX": ("sbuf", [128, 13360], BF), "X": ("sbuf", [128, 4240], BF),
    "K0": ("sbuf", [128, 1040], BF), "K1": ("sbuf", [128, 1040], BF), "K2": ("sbuf", [128, 1040], BF),
    "KB0": ("sbuf", [128, 1024], BF), "KB1": ("sbuf", [128, 1024], BF), "CV0": ("sbuf", [128, 1024], BF), "CV1": ("sbuf", [128, 1024], BF),
    "Q": ("sbuf", [128, 1024], BF), "CL": ("sbuf", [128, 512], BF),
    "P0": ("sbuf", [128, 1040], BF), "M0": ("sbuf", [128, 2048], BF), "M1": ("sbuf", [128, 2048], BF),
    "W0": ("sbuf", [128, 2064], BF), "W1": ("sbuf", [128, 2064], BF), "W2": ("sbuf", [128, 2064], BF),
    "LK": ("sbuf", [128, 128], I32), "LC": ("sbuf", [128, 64], I32), "LZ": ("sbuf", [128, 64], I32),
    "LT": ("sbuf", [128, 64], I32), "LP": ("sbuf", [128, 64], I32),
    "NI": ("sbuf", [128, 256], I32), "NH": ("sbuf", [128, 256], BF), "NL": ("sbuf", [128, 256], BF),
    "YN": ("sbuf", [128, 256], F32),
    "U": ("sbuf", [128, 64 * 26], U16), "TF": ("sbuf", [128, 64 * 128], F32),
    "PI": ("sbuf", [128, 4], I32), "CF": ("sbuf", [128, 32], F32),
    "IU": ("sbuf", [128, 144], F32), "IG": ("sbuf", [128, 128], F32), "IK": ("sbuf", [128, 128], F32),
    "IV": ("sbuf", [128, 128], F32), "IC": ("sbuf", [128, 8], F32),
    "Z": ("sbuf", [128, 144], BF), "Z2": ("sbuf", [128, 144], BF), "ZH": ("sbuf", [128, 144], F16),
    "G": ("sbuf", [128, 128], BF), "GN": ("sbuf", [128, 128], BF), "H1": ("sbuf", [128, 128], BF), "H": ("sbuf", [128, 128], BF),
    "ONE": ("sbuf", [128, 64], BF), "SG": ("sbuf", [128, 448], F32), "BEST": ("sbuf", [128, 448], F32),
    "HAS": ("sbuf", [128, 64], BF), "PRE": ("sbuf", [128, 64], BF), "JK": ("sbuf", [128, 512], BF),
    "BI": ("sbuf", [128, 128], I32), "LV": ("sbuf", [128, 72], F32), "PL": ("sbuf", [128, 72], F32),
    "MM": ("sbuf", [128, 128], BF), "EE": ("sbuf", [128, 128], F16),
    "CA": ("sbuf", [128, 8], F32),
    "CN0": ("sbuf", [128, 4], F32), "CN1": ("sbuf", [128, 4], F32), "CR0": ("sbuf", [128, 4], F32), "CR1": ("sbuf", [128, 4], F32),
    "SN0": ("sbuf", [128, 128], BF), "SN1": ("sbuf", [128, 128], BF), "RC0": ("sbuf", [128, 128], BF), "RC1": ("sbuf", [128, 128], BF),
    "pA": ("psum", [128, 512], F32), "pB": ("psum", [128, 512], F32), "pV": ("psum", [128, 512], F32), "pS": ("psum", [128, 512], F32),
    "pC": ("psum", [128, 512], F32), "pD": ("psum", [128, 512], F32), "pE": ("psum", [128, 512], F32), "pY": ("psum", [128, 512], F32),
}
SEMAPHORES = ["v", "a", "t", "p", "sent", "ac0", "ac1", "ad0", "ad1"] + ["d%d" % i for i in range(20)]
C = [(8 - k) * 8192.0 for k in range(8)]
CYC, GAT, SCA, PE, WAKE, DMA, BW, RIS, RLAT = 1.04, 1.56, 3.8, 0.52, 100.0, 2000.0, 250.0, 1000.0, 2500.0
SLACK = 40.0
PLAN = {}


def clash(x, y):
    for n, lo, hi in x:
        for m, lo2, hi2 in y:
            if n == m and lo < hi2 and lo2 < hi:
                return True
    return False


def plan(ops):
    n = len(ops)
    bk = [set(a for a, lo, hi in o["r"] + o["w"] if a in SCRATCH and SCRATCH[a][0] == "psum") for o in ops]
    dep = [[] for o in ops]
    for j, o in enumerate(ops):
        if o["q"] is None:
            dep[j].append(j - 1)
            continue
        for i in range(j):
            d = ops[i]
            if ((d["q"] != o["q"] or o["q"] == "t") and bk[i] & bk[j]) or clash(d["w"], o["r"]) or clash(d["w"], o["w"]) or clash(d["r"], o["w"]):
                dep[j].append(i)
    soft = [[i for i in range(j) if ops[i]["tag"] & ops[j]["after"]] for j in range(n)]
    rest = [0.0] * n
    for j in range(n - 1, -1, -1):
        rest[j] += ops[j]["cost"] + ops[j]["lat"]
        for i in dep[j] + soft[j]:
            rest[i] = max(rest[i], rest[j] + (WAKE if i in dep[j] else 0.0))
    left = [len(set(dep[j] + soft[j])) for j in range(n)]
    kids = [[] for o in ops]
    for j in range(n):
        for i in set(dep[j] + soft[j]):
            kids[i].append(j)
    free, fin, order = {}, [0.0] * n, []
    ready = [j for j in range(n) if left[j] == 0]
    can = [0.0] * n
    while ready:
        st = {j: max(free.get(ops[j]["q"], 0.0), can[j]) for j in ready}
        a = min(ready, key=lambda j: (st[j], j))
        j = max([x for x in ready if ops[x]["q"] == ops[a]["q"] and st[x] <= st[a] + SLACK], key=lambda x: (rest[x], -x))
        ready.remove(j)
        order.append(j)
        if ops[j]["q"] is not None:
            free[ops[j]["q"]] = st[j] + ops[j]["cost"]
        fin[j] = st[j] + ops[j]["cost"] + ops[j]["lat"]
        for k in kids[j]:
            pe = ops[j]["q"] == "t" and ops[k]["q"] == "t"
            can[k] = max(can[k], fin[j] + (0.0 if pe or ops[k]["q"] is None or j not in dep[k] else WAKE))
            left[k] -= 1
            if left[k] == 0:
                ready.append(k)
    clock, seq, key, pos, clk, at = {}, {}, [None] * n, [0] * n, [None] * n, [0] * n
    waits, mark = [[] for o in ops], [False] * n
    for x, j in enumerate(order):
        o = ops[j]
        at[j] = x
        if o["sem"] is None:
            seq[o["q"]] = seq.get(o["q"], 0) + 1
            key[j], pos[j] = o["q"], seq[o["q"]]
        else:
            key[j], pos[j] = o["sem"], 1
        if o["q"] is None:
            clk[j] = {key[j]: 1}
            continue
        ck = clock.setdefault(o["q"], {})
        for i in sorted(dep[j], key=lambda z: -at[z]):
            if ck.get(key[i], 0) >= pos[i] or (o["q"] == "t" and ops[i]["q"] == "t"):
                continue
            waits[j].append(i)
            mark[i] = True
            for k, val in clk[i].items():
                if ck.get(k, 0) < val:
                    ck[k] = val
        clk[j] = dict(ck)
        clk[j][key[j]] = pos[j]
    cnt, val = {}, [16] * n
    for j in order:
        if ops[j]["sem"] is None:
            cnt[key[j]] = cnt.get(key[j], 0) + (1 if mark[j] else 0)
            val[j] = cnt[key[j]]
    return order, [[(key[i], val[i]) for i in w] for w in waits], mark


def emit(g, T, ops):
    q = {"v": g.vector, "a": g.scalar, "t": g.tensor, "p": g, "s": g.sync}
    if "p" not in PLAN:
        PLAN["p"] = plan(ops)
    order, waits, mark = PLAN["p"]
    for j in order:
        o = ops[j]
        if o["q"] is None:
            continue
        for s, v in waits[j]:
            q[o["q"]].wait_ge(T.sem[s], v)
        ins = o["f"]()
        if o["kind"] == "dma":
            ins.then_inc(T.sem[o["sem"]], 16)
        elif o["kind"] == "op" and mark[j]:
            ins.then_inc(T.sem[o["q"]], 1)
    for j in order:
        if ops[j]["kind"] == "dma" and not mark[j]:
            q[ops[j]["q"]].wait_ge(T.sem[ops[j]["sem"]], 16)


def rank_program(g, core, T, topo):
    rank = T.rank_of(core)
    if rank is None:
        return
    dst = T.cores[(rank + 1) % len(T.cores)]
    rid, pid, _ = topo.addr(dst)
    mask = topo.mask(core, dst)
    ops = []
    nd, nt, nu, ns, np_ = [0], [0], [0], [0], {}

    def S(name, lo=0, hi=None, st=1, also=()):
        if hi is None:
            hi = SCRATCH[name][1][1]
        return (T[name][:, lo:hi:st] if st > 1 else T[name][:, lo:hi], [(name, lo, hi)] + list(also), (hi - lo + st - 1) // st, name, None)

    def N(name, lo, n, st):
        return S(name, lo, lo + (n - 1) * st + 1, st)

    def ind(w, o):
        return (w[0].indirect(o[0]), w[1], 16 * o[2], w[3], o[1])

    def tmp(n=64):
        nt[0] += n
        return S("TF", nt[0] - n, nt[0])

    def ptmp(bank, n=64):
        np_[bank] = np_.get(bank, 0) % 7 + 1
        return S(bank, 64 * np_[bank], 64 * np_[bank] + n)

    def lst(n=64):
        nu[0] += n
        return S("U", nu[0] - n, nu[0])

    def sub(x, lo, hi):
        name, a, b = x[1][0]
        return S(name, a + lo, a + hi)

    def add(q, f, r, w, cost, lat=0.0, kind="op", sem=None):
        ops.append({"q": q, "f": f, "r": [i for x in r for i in x[1]] + [i for x in r + w if x[4] for i in x[4]],
                    "w": [i for x in w for i in x[1]], "kind": kind, "sem": sem, "cost": cost, "lat": lat, "tag": set(), "after": set()})

    def after(*names):
        ops[-1]["after"].update(names)

    def tag(name):
        ops[-1]["tag"].add(name)

    def vc(out, a, per):
        if out[4]:
            return 50 + out[2] * SCA * CYC
        if a[4]:
            return 50 + a[2] * GAT * CYC
        return max(64, a[2] * per) * CYC

    def half(*xs):
        return 0.5 if all(SCRATCH[x[3]][2] in (BF, U16, F16) for x in xs) else 1.0

    def dma(q, out, in_, nbytes):
        e = {"s": g.sync, "a": g.scalar}[q]
        nd[0] += 1
        add(q, lambda: e.dma_start(out[0], in_[0]), [in_], [out], 60.0, DMA + nbytes / BW, "dma", "d%d" % (nd[0] - 1))

    def hbm(ap):
        return (ap, [], 0, None, None)

    def isap(x):
        return isinstance(x, tuple)

    def ts(out, in0, s1, op0, s2=None, op1=None):
        r = [in0] + [x for x in (s1, s2) if isap(x)]
        a1, a2 = (s1[0] if isap(s1) else s1), (s2[0] if isap(s2) else s2)
        if op1 is None:
            add("v", lambda: g.vector.tensor_scalar(out[0], in0[0], a1, None, op0), r, [out], vc(out, in0, half(out, in0)))
        else:
            add("v", lambda: g.vector.tensor_scalar(out[0], in0[0], a1, a2, op0, op1), r, [out], vc(out, in0, half(out, in0)))
        return out

    def tt(out, a, b, op):
        add("v", lambda: g.vector.tensor_tensor(out[0], a[0], b[0], op), [a, b], [out], vc(out, a, 1 if "p" in (a[3][0], b[3][0]) else 2))
        return out

    def cp(out, a):
        add("v", lambda: g.vector.tensor_copy(out[0], a[0]), [a], [out], vc(out, a, half(out, a)))
        return out

    def fill(out, c):
        add("v", lambda: g.vector.memset(out[0], c), [], [out], vc(out, out, half(out)))

    def scan(out, d0, d1, op0, op1):
        add("v", lambda: g.vector.tensor_tensor_scan(out[0], d0[0], d1[0], 0.0, op0, op1), [d0, d1], [out], vc(out, d0, half(out, d0, d1)))

    def act(out, a, func, bias=0.0, scale=1.0, acc=None):
        r = [a] + [x for x in (bias, scale) if isap(x)]
        b, s = (bias[0] if isap(bias) else bias), (scale[0] if isap(scale) else scale)
        if acc is None:
            add("a", lambda: g.scalar.activation(out[0], a[0], func, bias=b, scale=s), r, [out], vc(out, a, 1))
        else:
            add("a", lambda: g.scalar.activation(out[0], a[0], func, bias=b, scale=s, accum_out=acc[0]), r, [out, acc], vc(out, a, 1) + 20)
        return out

    def lin(out, a, scale, bias):
        return act(out, a, F.Identity, bias, scale)

    def mms(out, pairs, start=True, stop=True):
        def f():
            for i, (l, r) in enumerate(pairs):
                ins = g.tensor.matmul(out[0], l[0], r[0], start and i == 0, stop and i == len(pairs) - 1)
            return ins
        add("t", f, [x for p in pairs for x in p], [out], sum(max(64, r[2]) for l, r in pairs) * PE)

    def toL(out, name, lo, n, z="Z", start=True, stop=True):
        mms(out, [(S(z, 15 - i, 143 - i), N(name, lo + i, n, 16)) for i in range(16)], start, stop)

    def iota(out, pat, base, cm, flt=True):
        if flt:
            add("p", lambda: g.iota(out[0], pat, base, cm, allow_small_or_imprecise_dtypes=True), [], [out], 130 + 2 * CYC * out[2])
        else:
            add("p", lambda: g.iota(out[0], pat, base, cm), [], [out], 130 + 2 * CYC * out[2])
        tag("i%d" % len(ops))
        after("i%d" % (len(ops) - 1))

    def send(out, in_, sem):
        ns[0] += 1
        add("p", lambda: g.remote_dma(out[0], in_[0], T.sem[sem], T.sem.sent, pid, rid, mask), [in_], [], RIS, RLAT, "remote", "x%d" % ns[0])
        add(None, None, [], [out], 0.0, 0.0, "ext", sem)

    NY = [("NX0", 0, 1), ("NX1", 0, 1)]
    NXG, XG = S("NX", 0, 4112, 1, NY), S("X", 0, 4112)
    dma("s", S("LK", 64, 128), hbm(T.kr[:]), 32768)
    dma("s", S("K0", 0, 1024), hbm(T.ky[:]), 262144)
    dma("s", S("LK", 0, 64), hbm(T.kl[:]), 32768)
    dma("a", S("NI"), hbm(T.nxt[:]), 131072)
    for n, t_ in (("LC", T.cur), ("LZ", T.siz), ("LT", T.tgt), ("LP", T.par)):
        dma("a", S(n), hbm(t_[:]), 32768)
    iota(S("PI", 0, 1), [[0, 1]], 0, 1, False)
    iota(S("IV"), [[0, 2], [16, 64]], 0, 1)
    iota(S("IU"), [[1, 144]], -15, 0)
    iota(S("IG"), [[16, 8], [0, 16]], 0, 0)
    iota(S("IC"), [[-8192, 8]], 65536, 0)
    iota(S("K0", 1024, 1040), [[0, 16]], 255, 0)
    iota(S("NX", 0, 16), [[0, 16]], 0, 0)
    iota(S("P0", 1024, 1040), [[0, 16]], 0, 0)
    iota(S("M0", 0, 1024), [[0, 1024]], 0, 0)
    iota(S("K1", 1024, 1040), [[0, 16]], 255, 0)
    iota(S("X", 0, 16), [[0, 16]], 255, 0)
    for w in ("W0", "W1", "W2"):
        iota(S(w, 1536, 1552), [[0, 16]], 0, 0)
    iota(S("IK"), [[1, 128]], -1023, 0)
    iota(S("M1", 0, 1024), [[0, 1024]], 0, 0)
    iota(S("ONE"), [[0, 64]], 1, 0)
    iota(S("PL", 64, 72), [[0, 8]], 5000, 0)
    iota(S("LV", 64, 72), [[0, 8]], 0, 0)
    fill(S("NX", 16, 1040), 16.0)
    act(S("NX", 1040, 2064), S("NX", 16, 1040), F.Copy)
    act(S("NX", 2064, 2832), S("NX", 16, 784), F.Copy)
    fill(S("NX", 2832, 4112), 16.0)
    ts(S("PI", 1, 2), S("PI", 0, 1), 112, A.bitwise_and)
    ts(S("PI", 2, 3), S("PI", 0, 1), 15, A.bitwise_and)
    cp(S("CF", 0, 2), S("PI", 1, 3))
    pg, pm = S("CF", 0, 1), S("CF", 1, 2)
    r2 = ts(S("CF", 2, 3), pm, 2.0, A.is_equal)
    r01 = ts(S("CF", 3, 4), pm, 2.0, A.is_lt)
    SC = ts(S("CF", 5, 6), pm, 3.0, A.is_equal, r01, A.add)
    vid2 = ts(tmp(128), S("IV"), pg, A.subtract)
    vid = sub(vid2, 0, 64)
    act(S("CF", 8, 16), S("IC"), F.Identity, 0.0, r2)
    ts(S("Z"), S("IU"), pg, A.is_equal)
    cp(S("ZH"), S("Z"))
    act(S("Z2"), S("Z"), F.Identity, 0.0, r01)
    ts(S("G"), S("IG"), pg, A.is_equal)
    act(S("GN"), S("G"), F.Identity, 0.0, -1.0)
    add("p", lambda: g.affine_select(T.H1[:], T.GN[:], [[-1, 128]], A.is_gt, 0.0, 0, 1), [S("GN")], [S("H1")], 440.0)
    add("p", lambda: g.affine_select(T.H[:], T.H1[:], [[-1, 128]], A.not_equal, -1024.0, 0, 1), [S("H1")], [S("H")], 440.0)
    Nn = lin(tmp(), vid, 1.0, 1024.0)
    NV = lin(tmp(), vid, 1.0, 8224.0)
    kb = lin(tmp(8), sub(vid, 0, 8), 1.0, 0.5)
    dum = lin(tmp(8), sub(vid, 0, 8), 1.0, 4112.0)
    bank = ("pA", "pB")
    E0 = (232, 8)
    V0 = (239, 8)
    fill(N("pB", V0[0] - 1, 33, 7), 0.0)
    fill(N("pA", V0[1] - 2, 33, 7), 0.0)
    fill(N("pA", V0[1] - 1, 33, 7), 0.0)

    def BC(k):
        return S("CF", 8 + k, 9 + k)

    ku = cp(lst(128), S("LK"))
    cp(S("NH"), S("NI"))
    tag("nh")
    tt(S("NL"), S("NI"), S("NH"), A.subtract)
    tag("nl")
    filled = [("NX", 16, 4112)]
    dma("s", (T.NX[0:128:16, 16:4112], NY[0:1], 0, "NX", None), S("NH", also=filled), 65536)
    dma("s", (T.NX[1:128:16, 16:4112], NY[1:2], 0, "NX", None), S("NL", also=filled), 65536)
    dma("s", S("X", 16, 4112), (T.x[:], NY, 0, None, None), 1048576)
    c16 = ts(tmp(), S("LC"), 16.0, A.add)
    zl = ts(ptmp("pD"), S("LZ"), 0.0, A.is_gt)
    ul = tt(tmp(), zl, c16, A.mult)
    u0 = cp(lst(), ul)
    P = [S("P0"), S("W0", 512, 1552)]
    K = [S("K0"), S("K1"), S("K2")]
    for h in (0, 1):
        act(S("P0", 512 * h, 512 * h + 512), ind(NXG, sub(u0, 32 * h, 32 * h + 32)), F.Identity, BC(7), SC)
    toL(S("pC", 0, 64), "P0", 0, 64)
    na = act(tmp(), S("pC", 0, 64), F.Copy)
    x1 = ts(S("pE", 0, 128), S("LK"), 1024.0, A.is_equal)
    x2 = tt(S("pE", 128, 256), x1, vid2, A.mult)
    after("nl")
    LR = tt(tmp(128), x2, S("LK"), A.add)
    dR = tt(tmp(), sub(LR, 64, 128), Nn, A.subtract)
    dL = tt(tmp(), sub(LR, 0, 64), sub(LR, 64, 128), A.subtract)
    lt = tt(tmp(), S("LZ"), S("LT"), A.is_lt)
    par = cp(tmp(), S("LP"))
    acts = tt(tmp(), lt, par, A.is_gt)
    th = [lin(tmp(), par, -8192.0, 8192.0), lin(tmp(), par, 8192.0, 0.0)]
    cap = [lin(tmp(), par, -65536.0, 73728.0), lin(tmp(), par, 65536.0, 8192.0)]
    dz = ts(ptmp("pD"), S("LZ"), 0.0, A.is_equal)
    cx = tt(tmp(), tt(ptmp("pD"), dz, NV, A.mult), ul, A.add)
    da = tt(tmp(), ts(ptmp("pD"), S("LT"), 0.0, A.is_gt), lt, A.subtract)
    cur = c16
    LS = [[None] + [lst() for k in range(6)] for t in range(2)]

    def vote(t, acts):
        kb_, cv = "KB%d" % t, "CV%d" % t
        for h in (0, 1):
            act(S(kb_, 512 * h, 512 * h + 512), ind(K[t], sub(ku, 64 + 32 * h, 96 + 32 * h)), F.Copy)
            tt(S(cv, 512 * h, 512 * h + 512), ind(K[t], sub(ku, 32 * h, 32 * h + 32)), S(kb_, 512 * h, 512 * h + 512), A.is_le)
        toL(S("pV", 0, 64), cv, 0, 64)
        thv = ts(tmp(), acts, -90.0, A.mult, 99.0, A.add)
        rp = tt(tmp(), tt(ptmp("pD"), acts, dR, A.mult), Nn, A.add)
        s = tt(ptmp("pV"), S("pV", 0, 64), thv, A.is_ge)
        ml = tt(tmp(), tt(ptmp("pV"), s, dL, A.mult), rp, A.add)
        mu, ql = cp(lst(), ml), ts(lst(), ml, 1024.0, A.min)
        tag("ql%d" % t)
        return ml, ql, mu, tt(tmp(), ml, vid, A.subtract)

    def meld_a(t, v, h):
        ml, ql, mu, mlv = v
        if h == 0:
            act(S("Q"), ind(P[t], ql), F.Copy)
            toL(S("pS", 0, 64), "Q", 0, 64, stop=False)
        cp(ind(S("M%d" % t), sub(mu, 32 * h, 32 * h + 32)), sub(P[t], 512 * h, 512 * h + 512))
        after("ql%d" % t)

    def meld(t, v, cx, na):
        ml, ql, mu, mlv = v
        m = "M%d" % t
        toL(S("pS", 0, 64), m, 0, 64, start=False)
        s = S("pS", 0, 64)
        a = ts(ptmp("pS"), s, 8192.0, A.is_le, 4112.0, A.mult)
        e = tt(ptmp("pS"), s, th[t], A.is_gt)
        ne = tt(ptmp("pS"), s, th[t], A.is_le)
        sx = tt(tmp(), s, cap[t], A.min)
        no = cp(lst(), tt(tmp(), a, cx, A.add))
        su = ts(lst(), tt(tmp(), tt(ptmp("pS"), e, mlv, A.mult), vid, A.add), 1024.0, A.min)
        tag("su%d" % t)
        act(sub(K[t + 1], 0, 1024), ind(K[t], su), F.Copy)
        s1 = tt(tmp(), tt(ptmp("pS"), ne, na, A.mult), sx, A.max)
        ts(LS[t][1], s1, 8192.0, A.subtract)
        tag("s1%d" % t)
        tt(ind(S("NX", 0, None, 1, NY), no), S("Q"), S(m, 0, 1024), A.add)
        after("su%d" % t, "s1%d" % t, "snd%d" % (t - 1))
        for h in (0, 1):
            lin(N(bank[h], E0[h] + 6, 32, 7), sub(s1, 32 * h, 32 * h + 32), 1.0, C[1] - 8192.0)
        return act(ptmp("pY"), s1, F.Relu, 8193.0, -1.0)

    def walk(t):
        def cmp(out, k, h):
            tt(out, ind(XG, sub(LS[t][k], 32 * h, 32 * h + 32)), sub(K[t + 1], 512 * h, 512 * h + 512), A.is_lt)

        def cvt(k, h):
            ts(sub(LS[t][k], 32 * h, 32 * h + 32), N(bank[h], E0[h] + 7 - k, 32, 7), C[k], A.subtract)
        for k in range(1, 7):
            w = "W%d" % (k % 3)
            if k == 6 and t == 1:
                cvt(6, 0)
                cvt(6, 1)
                cmp(S(w, 1552, 2064), 6, 0)
                tag("a6")
                toL(N("pB", V0[0], 32, 7), w, 1552, 32)
                cmp(S(w, 0, 512), 5, 1)
                after("a6")
                toL(N("pA", V0[1], 32, 7), w, 0, 32)
                break
            for h in (0, 1):
                if k > 1:
                    cvt(k, h)
                act(S(w, 512 + 512 * h, 1024 + 512 * h), ind(NXG, sub(LS[t][k], 32 * h, 32 * h + 32)), F.Identity, BC(k + 1), SC)
                if h == 0:
                    if k > 1:
                        cmp(S(w, 0, 512), k - 1, 1)
                    lo = 0 if k > 1 else 32
                    toL(N("pA", 14 - k + 7 * lo, 64 - lo, 7), w, 16 * lo, 64 - lo)
                else:
                    cmp(S(w, 1552, 2064), k, 0)
                    toL(N("pB", 14 - k, 65, 7), w, 1024, 65)
        cmp(S("CL"), 6, 1)
        toL(S("pV", 0, 32), "CL", 0, 32)

    def exchange_a(t):
        for h in (0, 1):
            act(S("SG", 224 * h, 224 * h + 224), S(bank[1 - h], V0[h] - 1 - h, V0[h] + 223 - h), F.Relu, -8.0 * 65536, 65536.0)
        for h in (1, 0):
            c = (224 * h, 224 * h + 224)
            scan(S("BEST", *c), S("SG", *c), S(bank[h], E0[h], E0[h] + 224), A.max, A.min)
        ba, bb, v6 = N("BEST", 6, 32, 7), N("BEST", 230, 32, 7), S("pV", 0, 32)
        ts(S("HAS", 0, 32), ba, C[6], A.is_ge)
        thr = ts(tmp(32), bb, C[6], A.is_lt, 9.0, A.mult)
        tt(S("HAS", 32, 64), v6, thr, A.is_ge)
        scan(S("PRE"), S("ONE"), S("HAS"), A.mult, A.add)
        tag("pre%d" % t)

    def exchange_b(t):
        ba, bb, v6 = N("BEST", 6, 32, 7), N("BEST", 230, 32, 7), S("pV", 0, 32)
        e6 = act(tmp(32), N("pB", E0[1] + 1, 32, 7), F.Copy)
        mms(S("pC", 0, 64), [(S("G"), S("PRE"))])
        mms(S("pD", 0, 64), [(S("G"), S("PRE")), (S("H"), S("HAS"))])
        cn, cr, sn, rc = S("CN%d" % t), S("CR%d" % t), S("SN%d" % t), S("RC%d" % t)
        act(cn, S("pC", 60, 64), F.Copy)
        tag("cn%d" % t)
        send(cr, cn, "ac%d" % t)
        for j in range(8):
            act(S("JK", 64 * j, 64 * j + 64), S("pC", 0, 64), F.Sign, sub(kb, j, j + 1), -1.0, S("CA", j, j + 1))
            after("cn%d" % t)
        cp(S("BI", 0, 32), ba)
        k6 = tt(ptmp("pV", 32), ts(ptmp("pV", 32), v6, 9.0, A.is_ge), e6, A.mult)
        tt(S("BI", 32, 64), k6, bb, A.max)
        cp(S("PL", 0, 64), S("pD", 0, 64))
        ts(S("BI", 64, 128), S("BI", 0, 64), 8191, A.bitwise_and)
        ts(S("LV", 0, 64), S("BI", 64, 128), 2064.0, A.subtract)
        cu = ts(lst(8), S("CA"), 0.5, A.mult, 32.0, A.add)
        tt(S("MM"), ind(S("PL"), cu), S("IK"), A.is_equal)
        tt(S("EE"), ind(S("LV"), cu), S("MM"), A.mult)
        toL(S("pE", 0, 8), "EE", 0, 8, "ZH")
        tag("pe%d" % t)
        eu = ts(lst(8), S("pE", 0, 8), 2064.0, A.add)
        cp(sn, ind(XG, eu))
        tag("snd%d" % t)
        send(rc, sn, "ad%d" % t)
        ef = lin(tmp(8), S("pE", 0, 8), 1.0, 2064.0)
        cm = tt(tmp(4), cn, cr, A.min)
        o = tt(tmp(8), tt(tmp(8), ts(tmp(8), sub(vid, 0, 8), sub(cm, 3, 4), A.is_ge), dum, A.mult), ef, A.max)
        cp(ind(S("X"), cp(lst(8), o)), rc)

    v0 = vote(0, acts)
    meld_a(0, v0, 0)
    meld_a(0, v0, 1)
    dead = meld(0, v0, cx, na)
    acts = tt(tmp(), tt(ptmp("pY"), tt(ptmp("pY"), dead, da, A.mult), lt, A.add), par, A.mult)
    v1 = vote(1, acts)
    dn, dc = tt(ptmp("pY"), dead, NV, A.mult), tt(ptmp("pY"), dead, cur, A.mult)
    walk(0)
    na = tmp()
    for h in (0, 1):
        act(sub(na, 32 * h, 32 * h + 32), N(bank[h], E0[h], 32, 7), F.Copy)
    s6 = cp(tmp(), LS[0][6])
    cx, cur = tt(tmp(), dn, s6, A.add), tt(tmp(), dc, s6, A.add)
    meld_a(1, v1, 0)
    exchange_a(0)
    meld_a(1, v1, 1)
    after("pre0")
    exchange_b(0)
    dead = meld(1, v1, cx, na)
    dma("s", hbm(T.yk[:]), S("K2", 0, 1024), 262144)
    dc = tt(ptmp("pY"), dead, cur, A.mult)
    walk(1)
    yc = tt(tmp(), dc, ts(tmp(), LS[1][6], 16.0, A.subtract), A.add)
    dma("s", hbm(T.yc[:]), yc, 32768)
    exchange_a(1)
    exchange_b(1)
    mms(S("pS", 0, 256), [(S("Z2", 15 - i, 143 - i), S("NX", 16 + 256 * i, 272 + 256 * i, 1, NY)) for i in range(16)])
    after("pe1")
    act(S("YN"), S("pS", 0, 256), F.Copy)
    dma("a", hbm(T.yn[:]), S("YN"), 131072)
    dma("s", hbm(T.yx[:]), S("X", 16, 4112), 1048576)
    emit(g, T, ops)
    g.wait_ge(T.sem.sent, ns[0] * len(topo.engines(core, dst)))
